import numpy as np, ml_dtypes
CORES = [3,5,19,21,35,37,51,53,67,69]
N = 10
DEG, TK, TIMES = 3, 512, 3
MASK = [[9,0,1],[0,1,2],[1,2,3],[2,3,4],[3,4,5],[4,5,6],[5,6,7],[6,7,8],[7,8,9],[8,9,0]]
def setup_inputs(rng):
    return {"x": rng.standard_normal((N, 128, TK), dtype=np.float32).astype(ml_dtypes.bfloat16), "w": (rng.standard_normal((N, 128, DEG * 128), dtype=np.float32) / np.float32(np.sqrt(128 * DEG / 2))).astype(ml_dtypes.bfloat16)}
def setup_inputs_big(rng):
    d = setup_inputs(rng)
    for k in ("x",): d[k] = (d[k].astype(np.float32) * 1048576.0).astype(d[k].dtype)
    return d
def setup_inputs_small(rng):
    d = setup_inputs(rng)
    for k in ("x",): d[k] = (d[k].astype(np.float32) * (1 / 1048576.0)).astype(d[k].dtype)
    return d
def setup_inputs_apart(rng):
    d = setup_inputs(rng)
    f = (10.0 ** rng.permutation(np.linspace(-1.5, 1.5, N))).astype(np.float32).reshape(N, 1, 1)
    for k in ("x",): d[k] = (d[k].astype(np.float32) * f).astype(d[k].dtype)
    return d
def reference(x, w):
    X, W = x.astype(np.float64), w.astype(np.float64)
    h = list(X)
    for _ in range(TIMES):
        h = [sum(W[r][:, 128 * i:128 * i + 128].T @ h[j] for i, j in enumerate(MASK[r])) for r in range(N)]
    return {"y": np.stack(h).astype(ml_dtypes.bfloat16)}

@@ -1,0 +1,121 @@
+from concourse.bass import DstId, RemoteDMATransfer
+
+P = 128
+DEG, TK, TIMES = 3, 512, 3
+C = 2
+CW = TK // C
+NBANK = min(8, TIMES * C)
+
+SCRATCH = {"wt": ("sbuf", [P, DEG * P], "bfloat16")}
+SEMAPHORES = ["ldw", "sent"]
+for _c in range(C):
+    SEMAPHORES += ["ldx%d" % _c, "st%d" % _c]
+    for _t in range(TIMES + 1):
+        SCRATCH["h%d_%d" % (_t, _c)] = ("sbuf", [P, CW], "bfloat16")
+    for _t in range(1, TIMES + 1):
+        SEMAPHORES += ["mm%d_%d" % (_t, _c), "cp%d_%d" % (_t, _c)]
+    for _t in range(TIMES):
+        for _i in range(DEG):
+            SCRATCH["l%d_%d_%d" % (_t, _i, _c)] = ("sbuf", [P, CW], "bfloat16")
+            SEMAPHORES.append("a%d_%d_%d" % (_t, _i, _c))
+for _b in range(NBANK):
+    SCRATCH["ps%d" % _b] = ("psum", [P, 512], "float32")
+
+
+def _bits(m):
+    return [b for b in range(m.bit_length()) if (m >> b) & 1]
+
+
+def _plan(r, T, topo):
+    tbl = T.tables["MASK"]
+    src = T.cores[r]
+    outs = [(q, i) for q in range(len(T.cores)) for i, j in enumerate(tbl[q]) if j == r and q != r]
+    if not outs:
+        return []
+    for q, i in outs:
+        assert topo.may_write(src, T.cores[q])
+    allowed = [_bits(topo.mask(src, T.cores[q])) for q, i in outs]
+    order = sorted(range(len(outs)), key=lambda k: len(allowed[k]))
+    for per in [d for d in range(max(len(a) for a in allowed), 0, -1) if P % d == 0]:
+        used, got = set(), {}
+        for k in order:
+            free = [b for b in allowed[k] if b not in used][:per]
+            if len(free) < per:
+                break
+            used.update(free)
+            got[k] = free
+        if len(got) == len(outs):
+            return [(outs[k][0], outs[k][1], sum(1 << b for b in got[k]), per) for k in range(len(outs))]
+    raise ValueError("no disjoint engine sets")
+
+
+def rank_program(g, core, T, topo):
+    r = T.rank_of(core)
+    if r is None:
+        return
+    S = T.sem
+    row = T.tables["MASK"][r]
+    dmaq = [g.sync, g.scalar]
+
+    for c in range(C):
+        dmaq[c % 2].dma_start(T["h0_%d" % c][:], T.x[:, c * CW:(c + 1) * CW]).then_inc(S["ldx%d" % c], 16)
+    g.sync.dma_start(T.wt[:], T.w[:]).then_inc(S.ldw, 16)
+
+    plan = _plan(r, T, topo)
+    sent = 0
+    for t in range(TIMES):
+        for c in range(C):
+            if t == 0:
+                g.wait_ge(S["ldx%d" % c], 16)
+            else:
+                g.wait_ge(S["cp%d_%d" % (t, c)], 1)
+            trs = []
+            for q, i, m, n in plan:
+                rid, pid, _se = topo.addr(T.cores[q])
+                trs.append(RemoteDMATransfer(dst_ids=[DstId(rid=rid, pnc=pid)], dma_engine_mask=m,
+                                             remote_sem=S["a%d_%d_%d" % (t, i, c)],
+                                             src=T["h%d_%d" % (t, c)][:], dst=T["l%d_%d_%d" % (t, i, c)][:]))
+                sent += n
+            if trs:
+                g.remote_dma_fused(trs, local_sem=S.sent)
+
+    arrive = {}
+    for i, j in enumerate(row):
+        if j != r:
+            arrive[i] = [n for q, i2, m, n in _plan(j, T, topo) if q == r and i2 == i][0]
+    own = [i for i, j in enumerate(row) if j == r]
+    far = sorted(arrive, key=lambda i: topo.chip(T.cores[row[i]]) != topo.chip(core))
+    seq = own + far
+    g.tensor.wait_ge(S.ldw, 16)
+    for t in range(1, TIMES + 1):
+        for part in (own, far):
+            for c in range(C):
+                ps = T["ps%d" % (((t - 1) * C + c) % NBANK)][:, 0:CW]
+                if part is own and own:
+                    if t == 1:
+                        g.tensor.wait_ge(S["ldx%d" % c], 16)
+                    else:
+                        g.tensor.wait_ge(S["cp%d_%d" % (t - 1, c)], 1)
+                for i in part:
+                    if part is own:
+                        rhs = T["h%d_%d" % (t - 1, c)][:]
+                    else:
+                        g.tensor.wait_ge(S["a%d_%d_%d" % (t - 1, i, c)], arrive[i])
+                        rhs = T["l%d_%d_%d" % (t - 1, i, c)][:]
+                    mm = g.tensor.matmul(ps, T.wt[:, i * P:(i + 1) * P], rhs, i == seq[0], i == seq[-1])
+                    if i == seq[-1]:
+                        mm.then_inc(S["mm%d_%d" % (t, c)], 1)
+
+    for t in range(1, TIMES + 1):
+        for c in range(C):
+            g.vector.wait_ge(S["mm%d_%d" % (t, c)], 1)
+            g.vector.tensor_copy(T["h%d_%d" % (t, c)][:],
+                                 T["ps%d" % (((t - 1) * C + c) % NBANK)][:, 0:CW]).then_inc(S["cp%d_%d" % (t, c)], 1)
+
+    for c in range(C):
+        dmaq[c % 2].wait_ge(S["cp%d_%d" % (TIMES, c)], 1)
+        dmaq[c % 2].dma_start(T.y[:, c * CW:(c + 1) * CW], T["h%d_%d" % (TIMES, c)][:]).then_inc(S["st%d" % c], 16)
+    for c in range(C):
+        dmaq[c % 2].wait_ge(S["st%d" % c], 16)
+    if sent:
+        g.wait_ge(S.sent, sent)

@@ -2,8 +2,9 @@ from concourse.bass import DstId, RemoteDMATransfer
 
 P = 128
 DEG, TK, TIMES = 3, 512, 3
-C = 2
-CW = TK // C
+BLK = [128, 128, 128, 128]
+C = len(BLK)
+OFF = [sum(BLK[:c]) for c in range(C)]
 NBANK = min(8, TIMES * C)
 
 SCRATCH = {"wt": ("sbuf", [P, DEG * P], "bfloat16")}
@@ -11,12 +12,12 @@ SEMAPHORES = ["ldw", "sent"]
 for _c in range(C):
     SEMAPHORES += ["ldx%d" % _c, "st%d" % _c]
     for _t in range(TIMES + 1):
-        SCRATCH["h%d_%d" % (_t, _c)] = ("sbuf", [P, CW], "bfloat16")
+        SCRATCH["h%d_%d" % (_t, _c)] = ("sbuf", [P, BLK[_c]], "bfloat16")
     for _t in range(1, TIMES + 1):
         SEMAPHORES += ["mm%d_%d" % (_t, _c), "cp%d_%d" % (_t, _c)]
     for _t in range(TIMES):
         for _i in range(DEG):
-            SCRATCH["l%d_%d_%d" % (_t, _i, _c)] = ("sbuf", [P, CW], "bfloat16")
+            SCRATCH["l%d_%d_%d" % (_t, _i, _c)] = ("sbuf", [P, BLK[_c]], "bfloat16")
             SEMAPHORES.append("a%d_%d_%d" % (_t, _i, _c))
 for _b in range(NBANK):
     SCRATCH["ps%d" % _b] = ("psum", [P, 512], "float32")
@@ -58,8 +59,8 @@ def rank_program(g, core, T, topo):
     dmaq = [g.sync, g.scalar]
 
     for c in range(C):
-        dmaq[c % 2].dma_start(T["h0_%d" % c][:], T.x[:, c * CW:(c + 1) * CW]).then_inc(S["ldx%d" % c], 16)
-    g.sync.dma_start(T.wt[:], T.w[:]).then_inc(S.ldw, 16)
+        dmaq[c % 2].dma_start(T["h0_%d" % c][:], T.x[:, OFF[c]:OFF[c] + BLK[c]]).then_inc(S["ldx%d" % c], 16)
+    dmaq[C % 2].dma_start(T.wt[:], T.w[:]).then_inc(S.ldw, 16)
 
     plan = _plan(r, T, topo)
     sent = 0
@@ -90,7 +91,7 @@ def rank_program(g, core, T, topo):
     for t in range(1, TIMES + 1):
         for part in (own, far):
             for c in range(C):
-                ps = T["ps%d" % (((t - 1) * C + c) % NBANK)][:, 0:CW]
+                ps = T["ps%d" % (((t - 1) * C + c) % NBANK)][:, 0:BLK[c]]
                 if part is own and own:
                     if t == 1:
                         g.tensor.wait_ge(S["ldx%d" % c], 16)
@@ -110,11 +111,11 @@ def rank_program(g, core, T, topo):
         for c in range(C):
             g.vector.wait_ge(S["mm%d_%d" % (t, c)], 1)
             g.vector.tensor_copy(T["h%d_%d" % (t, c)][:],
-                                 T["ps%d" % (((t - 1) * C + c) % NBANK)][:, 0:CW]).then_inc(S["cp%d_%d" % (t, c)], 1)
+                                 T["ps%d" % (((t - 1) * C + c) % NBANK)][:, 0:BLK[c]]).then_inc(S["cp%d_%d" % (t, c)], 1)
 
     for c in range(C):
         dmaq[c % 2].wait_ge(S["cp%d_%d" % (TIMES, c)], 1)
-        dmaq[c % 2].dma_start(T.y[:, c * CW:(c + 1) * CW], T["h%d_%d" % (TIMES, c)][:]).then_inc(S["st%d" % c], 16)
+        dmaq[c % 2].dma_start(T.y[:, OFF[c]:OFF[c] + BLK[c]], T["h%d_%d" % (TIMES, c)][:]).then_inc(S["st%d" % c], 16)
     for c in range(C):
         dmaq[c % 2].wait_ge(S["st%d" % c], 16)
     if sent:

from concourse.bass import DstId, RemoteDMATransfer

P = 128
DEG, TK, TIMES = 3, 512, 3
BLK = [128, 128, 128, 128]
C = len(BLK)
OFF = [sum(BLK[:c]) for c in range(C)]
NBANK = min(8, TIMES * C)

SCRATCH = {"wt": ("sbuf", [P, DEG * P], "bfloat16")}
SEMAPHORES = ["ldw", "sent"]
for _c in range(C):
    SEMAPHORES += ["ldx%d" % _c, "st%d" % _c]
    for _t in range(TIMES + 1):
        SCRATCH["h%d_%d" % (_t, _c)] = ("sbuf", [P, BLK[_c]], "bfloat16")
    for _t in range(1, TIMES + 1):
        SEMAPHORES += ["mm%d_%d" % (_t, _c), "cp%d_%d" % (_t, _c)]
    for _t in range(TIMES):
        for _i in range(DEG):
            SCRATCH["l%d_%d_%d" % (_t, _i, _c)] = ("sbuf", [P, BLK[_c]], "bfloat16")
            SEMAPHORES.append("a%d_%d_%d" % (_t, _i, _c))
for _b in range(NBANK):
    SCRATCH["ps%d" % _b] = ("psum", [P, 512], "float32")


def _bits(m):
    return [b for b in range(m.bit_length()) if (m >> b) & 1]


def _plan(r, T, topo):
    tbl = T.tables["MASK"]
    src = T.cores[r]
    outs = [(q, i) for q in range(len(T.cores)) for i, j in enumerate(tbl[q]) if j == r and q != r]
    if not outs:
        return []
    for q, i in outs:
        assert topo.may_write(src, T.cores[q])
    allowed = [_bits(topo.mask(src, T.cores[q])) for q, i in outs]
    order = sorted(range(len(outs)), key=lambda k: len(allowed[k]))
    for per in [d for d in range(max(len(a) for a in allowed), 0, -1) if P % d == 0]:
        used, got = set(), {}
        for k in order:
            free = [b for b in allowed[k] if b not in used][:per]
            if len(free) < per:
                break
            used.update(free)
            got[k] = free
        if len(got) == len(outs):
            return [(outs[k][0], outs[k][1], sum(1 << b for b in got[k]), per) for k in range(len(outs))]
    raise ValueError("no disjoint engine sets")


def rank_program(g, core, T, topo):
    r = T.rank_of(core)
    if r is None:
        return
    S = T.sem
    row = T.tables["MASK"][r]
    dmaq = [g.sync, g.scalar]

    for c in range(C):
        dmaq[c % 2].dma_start(T["h0_%d" % c][:], T.x[:, OFF[c]:OFF[c] + BLK[c]]).then_inc(S["ldx%d" % c], 16)
    dmaq[C % 2].dma_start(T.wt[:], T.w[:]).then_inc(S.ldw, 16)

    plan = _plan(r, T, topo)
    sent = 0
    for t in range(TIMES):
        for c in range(C):
            if t == 0:
                g.wait_ge(S["ldx%d" % c], 16)
            else:
                g.wait_ge(S["cp%d_%d" % (t, c)], 1)
            trs = []
            for q, i, m, n in plan:
                rid, pid, _se = topo.addr(T.cores[q])
                trs.append(RemoteDMATransfer(dst_ids=[DstId(rid=rid, pnc=pid)], dma_engine_mask=m,
                                             remote_sem=S["a%d_%d_%d" % (t, i, c)],
                                             src=T["h%d_%d" % (t, c)][:], dst=T["l%d_%d_%d" % (t, i, c)][:]))
                sent += n
            if trs:
                g.remote_dma_fused(trs, local_sem=S.sent)

    arrive = {}
    for i, j in enumerate(row):
        if j != r:
            arrive[i] = [n for q, i2, m, n in _plan(j, T, topo) if q == r and i2 == i][0]
    own = [i for i, j in enumerate(row) if j == r]
    far = sorted(arrive, key=lambda i: topo.chip(T.cores[row[i]]) != topo.chip(core))
    seq = own + far
    g.tensor.wait_ge(S.ldw, 16)
    for t in range(1, TIMES + 1):
        for part in (own, far):
            for c in range(C):
                ps = T["ps%d" % (((t - 1) * C + c) % NBANK)][:, 0:BLK[c]]
                if part is own and own:
                    if t == 1:
                        g.tensor.wait_ge(S["ldx%d" % c], 16)
                    else:
                        g.tensor.wait_ge(S["cp%d_%d" % (t - 1, c)], 1)
                for i in part:
                    if part is own:
                        rhs = T["h%d_%d" % (t - 1, c)][:]
                    else:
                        g.tensor.wait_ge(S["a%d_%d_%d" % (t - 1, i, c)], arrive[i])
                        rhs = T["l%d_%d_%d" % (t - 1, i, c)][:]
                    mm = g.tensor.matmul(ps, T.wt[:, i * P:(i + 1) * P], rhs, i == seq[0], i == seq[-1])
                    if i == seq[-1]:
                        mm.then_inc(S["mm%d_%d" % (t, c)], 1)

    for t in range(1, TIMES + 1):
        for c in range(C):
            g.vector.wait_ge(S["mm%d_%d" % (t, c)], 1)
            g.vector.tensor_copy(T["h%d_%d" % (t, c)][:],
                                 T["ps%d" % (((t - 1) * C + c) % NBANK)][:, 0:BLK[c]]).then_inc(S["cp%d_%d" % (t, c)], 1)

    for c in range(C):
        dmaq[c % 2].wait_ge(S["cp%d_%d" % (TIMES, c)], 1)
        dmaq[c % 2].dma_start(T.y[:, OFF[c]:OFF[c] + BLK[c]], T["h%d_%d" % (TIMES, c)][:]).then_inc(S["st%d" % c], 16)
    for c in range(C):
        dmaq[c % 2].wait_ge(S["st%d" % c], 16)
    if sent:
        g.wait_ge(S.sent, sent)
